import numpy as np
import ml_dtypes


def mxq(x, axis, fmt="e4m3"):
    dtype, down = {"e4m3": (ml_dtypes.float8_e4m3fn, 7), "e5m2": (ml_dtypes.float8_e5m2, 14)}[fmt]
    v = np.moveaxis(np.asarray(x, np.float32).astype(ml_dtypes.bfloat16).astype(np.float64), axis, -1)
    blocks = v.reshape(v.shape[:-1] + (-1, 32))
    amax = np.abs(blocks).max(-1, keepdims=True)
    byte = np.maximum(np.where(amax > 0, np.frexp(amax)[1] - 1 + 127, 0) - down, 1)
    scale = np.exp2(byte - 127.0)
    codes = (blocks / scale).astype(np.float32).astype(dtype).astype(np.float64)
    return np.moveaxis((codes * scale).reshape(v.shape), -1, axis)


WIDE = False


def mx_kscale(k):
    if not WIDE:
        return np.ones(k)
    levels = np.array([10, -10, 5, -5, 0])
    if k % 512:
        return np.exp2(np.random.permutation(np.resize(levels, k // 32))).repeat(32)
    a = np.empty((k // 512, 16))
    for p in range(k // 512):
        a[p, :8] = np.random.permutation(np.resize(levels, 8))
        for g in range(8):
            far = levels[np.abs(levels - a[p, g]) >= 10]
            a[p, g + 8] = far[np.random.randint(len(far))]
    return np.exp2(a.ravel()).repeat(32)


BF16 = ml_dtypes.bfloat16


def bf(x):
    return np.asarray(x, np.float32).astype(BF16)


def f64(x):
    return np.asarray(x).astype(np.float64)


E2M1 = np.array([0.0, 0.5, 1.0, 1.5, 2.0, 3.0, 4.0, 6.0, -0.0, -0.5, -1.0, -1.5, -2.0, -3.0, -4.0, -6.0])


def pack_weight(w, fmt):
    k, n = w.shape
    w = f64(bf(w)).reshape(k // 32, 32, n)
    amax = np.abs(w).max(1)
    if fmt == "e4m3":
        byte = np.frexp(amax)[1] - 1 + 127 - 7
    else:
        mant, ex = np.frexp(amax / 6.0)
        byte = np.where(mant > 0.5, ex, ex - 1) + 127
    byte = np.clip(np.where(amax > 0, byte, 1), 1, 254)
    scaled = (w * np.exp2(127.0 - byte)[:, None, :]).reshape(k, n).astype(np.float32)
    by_word = np.ascontiguousarray(scaled.reshape(k // 512, 128, 4, n).transpose(0, 1, 3, 2))
    if fmt == "e4m3":
        words = by_word.astype(ml_dtypes.float8_e4m3fn).view(np.uint8)
    else:
        c = by_word.astype(ml_dtypes.float4_e2m1fn).view(np.uint8) & 0xF
        words = c[..., 0::2] | (c[..., 1::2] << 4)
    return np.ascontiguousarray(words), np.ascontiguousarray(byte.astype(np.uint8).reshape(k // 512, 16, n))


def unpack_weight(words, scales, fmt):
    g, p, n, _ = words.shape
    if fmt == "e4m3":
        vals = np.ascontiguousarray(words).view(ml_dtypes.float8_e4m3fn).astype(np.float64)
    else:
        nib = np.empty((g, p, n, 4), np.uint8)
        nib[..., 0::2] = words & 0xF
        nib[..., 1::2] = words >> 4
        vals = E2M1[nib]
    vals = vals * np.repeat(np.exp2(scales.astype(np.float64) - 127.0), 8, axis=1)[..., None]
    return vals.transpose(0, 1, 3, 2).reshape(g * 512, n)
def pack4(w):
    words, scales = pack_weight(w, "e2m1")
    return words.reshape(words.shape[0], 128, -1), scales


def unpack4(words, scales):
    return unpack_weight(words.reshape(words.shape[0], 128, -1, 2), scales, "e2m1")


E4M3FN = np.array([(-1.0 if i & 128 else 1.0) * ((1.0 + (i & 7) / 8.0) * 2.0 ** (((i >> 3) & 15) - 7) if i & 120 else (i & 7) * 2.0 ** -9) for i in range(256)])


def e4m3fn_bytes(y):
    return np.clip(np.asarray(y, np.float64), -448.0, 448.0).astype(np.float32).astype(ml_dtypes.float8_e4m3fn).view(np.uint8)


def e4m3fn_values(b):
    return E4M3FN[b]


V, B, D, H, O = 2, 512, 512, 512, 512
C = 2 * H


def sigmoid(v):
    return 1.0 / (1.0 + np.exp(-v))


def project(xi, weight, bias):
    return sigmoid((xi @ weight) + bias) - 0.5


def draw0():
    s, t = mx_kscale(D), mx_kscale(C)
    x = bf(np.random.standard_normal((V, B, D)) * s)
    p = bf(np.random.standard_normal((V, D, H)) / np.sqrt(D) / s[:, None])
    b = bf(np.random.standard_normal((V, H)) * 0.3)
    g = bf((1.0 + 0.1 * np.random.standard_normal(C)) * t)
    wd_words, wd_scales = pack4(np.random.standard_normal((C, O)) * 4.0 / np.sqrt(C) / t[:, None])
    bd = bf(np.random.standard_normal(O) * 0.3)
    return {"x": x,
            "p": p,
            "b": b,
            "g": g,
            "wd_words": wd_words,
            "wd_scales": wd_scales,
            "bd": bd}


def core(x, p, b, g, wd_words, wd_scales, bd):
    xq = mxq(f64(x), 2, "e4m3")
    pq = mxq(f64(p), 1, "e4m3")
    bias, gain = f64(b), f64(g)
    m_0 = project(xq[0], pq[0], bias[0])
    m_1 = project(xq[1], pq[0], bias[0])
    s_0 = project(xq[0], pq[1], bias[1])
    s_1 = project(xq[1], pq[1], bias[1])
    c_0 = np.concatenate([m_0, s_0], axis=-1)
    c_1 = np.concatenate([m_1, s_1], axis=-1)
    q = mxq(np.stack([c_0, c_1], axis=0) * gain, 2, "e4m3")
    q_2 = np.concatenate([q[1][:, :H], q[0][:, H:]], axis=-1)
    q_3 = np.concatenate([q[0][:, :H], q[1][:, H:]], axis=-1)
    cq = np.stack([q[0], q[1], q_2, q_3], axis=0)
    return sigmoid((cq @ unpack4(wd_words, wd_scales)) + f64(bd))


def setup_inputs():
    drawn = draw0()
    full = np.asarray(drawn['x']).astype(np.float64)
    scale = (np.abs(full).reshape(2, 4, 128, 4, 128).max(axis=(2, 4)) / 448.0).astype(np.float32)
    given = {}
    for key, value in drawn.items():
        if key == 'x':
            given['x_bytes'] = e4m3fn_bytes(full / np.repeat(np.repeat(scale.astype(np.float64), 128, axis=1), 128, axis=2))
            given['x_scale'] = scale
        else:
            given[key] = value
    return given


def reference(x_bytes, x_scale, p, b, g, wd_words, wd_scales, bd):
    return core(e4m3fn_values(x_bytes) * np.repeat(np.repeat(x_scale.astype(np.float64), 128, axis=1), 128, axis=2), p, b, g, wd_words, wd_scales, bd)

@@ -1,0 +1,375 @@
+from contextlib import ExitStack
+
+import concourse.mybir as mybir
+from concourse.masks import make_identity
+
+F32 = mybir.dt.float32
+BF16 = mybir.dt.bfloat16
+I32 = mybir.dt.int32
+U32 = mybir.dt.uint32
+U8 = mybir.dt.uint8
+FP8 = mybir.dt.float8_e4m3fn
+FP8X4 = mybir.dt.float8_e4m3fn_x4
+FP4X4 = mybir.dt.float4_e2m1fn_x4
+ACT = mybir.ActivationFunctionType
+MULT = mybir.AluOpType.mult
+ADD = mybir.AluOpType.add
+
+P = 128
+T4 = 4
+V = 2
+B = 512
+D = 512
+H = 512
+O = 512
+PARTS = ((0, 0), (1, 1), (1, 0), (0, 1))
+
+FLOPS = 2 * (V * V * B * D * H + len(PARTS) * B * 2 * H * O)
+
+
+def tile_switchtabmutualsalientswap_d2p_kernel(tc, x_bytes, x_scale, p, b, g, wd_words, wd_scales, bd, out):
+    nc = tc.nc
+    with ExitStack() as ctx:
+        keep = ctx.enter_context(tc.tile_pool(name="keep", bufs=1))
+        wide = ctx.enter_context(tc.tile_pool(name="wide", bufs=4))
+        work = ctx.enter_context(tc.tile_pool(name="work", bufs=2))
+        outs = ctx.enter_context(tc.tile_pool(name="outs", bufs=4))
+        ps1 = ctx.enter_context(tc.psum_pool(name="ps1", bufs=4))
+        ps2 = ctx.enter_context(tc.psum_pool(name="ps2", bufs=4))
+        ctx.enter_context(tc.manual_schedule())
+
+        def kept(shape, dtype, label):
+            made = keep.tile(shape, dtype, name=label, align_bytes=64)
+            return made
+
+        warm = kept([P, 1], F32, "warm")
+        nc.gpsimd.memset(warm[:], 0.0)
+        warmed = kept([P, 1], F32, "warmed")
+        nc.scalar.activation(out=warmed[:], in_=warm[:], func=ACT.Sigmoid)
+        ident = kept([P, P], F32, "ident")
+        make_identity(nc, ident[:])
+        identb = kept([P, P], BF16, "identb")
+        nc.gpsimd.tensor_copy(out=identb[:], in_=ident[:])
+        wds = kept([P, 2, O], U8, "wds")
+        nc.gpsimd.memset(wds[:].rearrange("q g n -> q (g n)").bitcast(I32), 0)
+
+        xs = kept([P, V * 16], F32, "xs")
+        nc.scalar.dma_start(out=xs[:], in_=x_scale.rearrange("a i j -> (a i j)").partition_broadcast(P))
+        braw = kept([P, V, T4], BF16, "braw")
+        nc.gpsimd.dma_start(out=braw[:], in_=b.rearrange("a (q t) -> q a t", t=T4))
+        graw = kept([P, 2, T4], BF16, "graw")
+        nc.gpsimd.dma_start(out=graw[:], in_=g.rearrange("(a q t) -> q a t", a=2, t=T4))
+
+        xb = {}
+
+        def load_x(a, h):
+            tile = kept([P, 2, D], U8, "xb%d%d" % (a, h))
+            nc.sync.dma_start(out=tile[:], in_=x_bytes[a, 256 * h : 256 * (h + 1), :].rearrange("(i q) k -> q i k", q=P))
+            xb[a, h] = tile
+
+        praw = {}
+
+        def load_p(w):
+            tile = kept([P, T4, H], BF16, "praw%d" % w)
+            nc.sync.dma_start(out=tile[:], in_=p[w].rearrange("(q j) c -> q j c", j=T4))
+            praw[w] = tile
+
+        load_x(0, 0)
+        load_x(0, 1)
+        load_p(0)
+        load_p(1)
+        load_x(1, 0)
+        load_x(1, 1)
+        wdw = kept([P, 2, 2 * O], U8, "wdw")
+        nc.sync.dma_start(out=wdw[:].bitcast(I32), in_=wd_words.bitcast(I32).rearrange("g q n -> q g n"))
+        for quad in range(4):
+            nc.sync.dma_start(
+                out=wds[32 * quad : 32 * quad + 4, :, :].bitcast(I32),
+                in_=wd_scales[:, 4 * quad : 4 * quad + 4, :].bitcast(I32).rearrange("g q n -> q g n"),
+            )
+        bdt = kept([P, O], BF16, "bdt")
+        nc.sync.dma_start(out=bdt[:], in_=bd.partition_broadcast(P))
+
+        bh = kept([P, V * T4], F32, "bh")
+        nc.gpsimd.tensor_scalar(out=bh[:], in0=braw[:].rearrange("q a t -> q (a t)"), scalar1=0.5, scalar2=0.0, op0=MULT, op1=ADD)
+        gh = kept([P, 2 * T4], F32, "gh")
+        nc.gpsimd.tensor_scalar(out=gh[:], in0=graw[:].rearrange("q a t -> q (a t)"), scalar1=0.5, scalar2=0.0, op0=MULT, op1=ADD)
+
+        xw = {}
+        xg = {}
+        xc = {}
+        xsc = {}
+        pg = {}
+        pc = {}
+        psc = {}
+        for a in range(V):
+            xg[a] = kept([P, B, T4], BF16, "xg%d" % a)
+            xc[a] = kept([P, B], U32, "xc%d" % a)
+            xsc[a] = kept([P, B], U8, "xsc%d" % a)
+            pg[a] = kept([P, T4 * P * T4], BF16, "pg%d" % a)
+            pc[a] = kept([P, H], U32, "pc%d" % a)
+            psc[a] = kept([P, H], U8, "psc%d" % a)
+            for h in range(2):
+                xw[a, h] = kept([P, 2, D], BF16, "xw%d%d" % (a, h))
+        qc = {}
+        qs = {}
+        for a in range(V):
+            for w in range(2):
+                qc[a, w] = kept([P, B], U32, "qc%d%d" % (a, w))
+                qs[a, w] = kept([P, B], U8, "qs%d%d" % (a, w))
+
+        def widen(a, h, i, engine):
+            for j in range(4):
+                cols = slice(P * j, P * (j + 1))
+                at = 16 * a + 4 * (2 * h + i) + j
+                src = xb[a, h][:, i, cols].bitcast(FP8)
+                dst = xw[a, h][:, i, cols]
+                if engine == "v":
+                    nc.vector.tensor_scalar(out=dst, in0=src, scalar1=xs[:, at : at + 1], scalar2=None, op0=MULT)
+                else:
+                    nc.scalar.activation(out=dst, in_=src, func=ACT.Copy, scale=xs[:, at : at + 1])
+
+        turned = {}
+
+        def turn(a, h):
+            bank = ps2.tile([P, 2, 2, P], F32, name="bank2")
+            for i in range(2):
+                words = xw[a, h][:, i, :].bitcast(F32)
+                for u in range(2):
+                    nc.tensor.transpose(bank[:, i, u, :], words[:, u : D // 2 : 2], ident[:])
+            turned[a, h] = bank
+
+        def empty(a, h, engine):
+            words = xg[a][:].rearrange("q n t -> q (n t)").bitcast(F32)
+            dst = words[:, 512 * h : 512 * (h + 1)].rearrange("q (i r u) -> q i r u", i=2, u=2)
+            src = turned[a, h][:].rearrange("q i u r -> q i r u")
+            if engine == "v":
+                nc.vector.tensor_copy(out=dst, in_=src)
+            else:
+                nc.scalar.copy(out=dst, in_=src)
+
+        def quant_x(a, h0, h1):
+            cols = slice(256 * h0, 256 * h1)
+            nc.vector.quantize_mx(
+                out=xc[a][:, cols].bitcast(FP8X4),
+                scales=xsc[a][:, cols],
+                in_=xg[a][:].rearrange("q n t -> q (n t)")[:, 1024 * h0 : 1024 * h1],
+            )
+
+        def interleave(w, t0, t1, engine):
+            dst = pg[w][:].rearrange("q (t m j) -> q t m j", t=T4, j=T4)[:, t0:t1]
+            src = praw[w][:].rearrange("q j (m t) -> q t m j", t=T4)[:, t0:t1]
+            if engine == "v":
+                nc.vector.tensor_copy(out=dst, in_=src)
+            else:
+                nc.scalar.copy(out=dst, in_=src)
+
+        def quant_p(w, t0, t1):
+            cols = slice(P * t0, P * t1)
+            nc.vector.quantize_mx(
+                out=pc[w][:, cols].bitcast(FP8X4), scales=psc[w][:, cols], in_=pg[w][:, T4 * P * t0 : T4 * P * t1]
+            )
+
+        th = {}
+
+        def project(a, w, t, h0=0, h1=2):
+            if t == 0 and h0 == 0:
+                parts = wide.tile([P, T4, B], F32, name="th")
+                th[a, w] = parts
+            rows = slice(256 * h0, 256 * h1)
+            acc = ps1.tile([P, B], F32, name="bank1")
+            cols = slice(P * t, P * (t + 1))
+            nc.tensor.matmul_mx(
+                out=acc[:, 0 : 256 * (h1 - h0)],
+                lhsT=pc[w][:, cols].bitcast(FP8X4),
+                lhsT_scale=psc[w][:, cols],
+                rhs=xc[a][:, rows].bitcast(FP8X4),
+                rhs_scale=xsc[a][:, rows],
+                start=True,
+                stop=True,
+            )
+            at = T4 * w + t
+            nc.scalar.activation(
+                out=th[a, w][:, t, rows],
+                in_=acc[:, 0 : 256 * (h1 - h0)],
+                func=ACT.Tanh,
+                bias=bh[:, at : at + 1],
+                scale=0.5,
+            )
+
+        qg = {}
+
+        def gain(a, w, h):
+            if h == 0:
+                made = work.tile([P, B, T4], BF16, name="qg", align_bytes=64)
+                qg[a, w] = made
+            rows = slice(256 * h, 256 * (h + 1))
+            nc.vector.tensor_tensor(
+                out=qg[a, w][:, rows, :],
+                in0=th[a, w][:, :, rows].rearrange("q t n -> q n t"),
+                in1=gh[:, T4 * w : T4 * (w + 1)].unsqueeze(1).to_broadcast([P, 256, T4]),
+                op=MULT,
+            )
+
+        def quant_q(a, w, h0, h1):
+            cols = slice(256 * h0, 256 * h1)
+            nc.vector.quantize_mx(
+                out=qc[a, w][:, cols].bitcast(FP8X4),
+                scales=qs[a, w][:, cols],
+                in_=qg[a, w][:].rearrange("q n t -> q (n t)")[:, 1024 * h0 : 1024 * h1],
+            )
+
+        zs = {}
+
+        def decode(j, i, slot):
+            if slot == 0:
+                made = outs.tile([P, 2, O], F32, name="z")
+                zs[j] = made
+            if j in (1, 3) and slot == 1:
+                acc = ps1.tile([P, O], F32, name="bank1")
+            else:
+                acc = ps2.tile([P, O], F32, name="bank2")
+            cols = slice(P * i, P * (i + 1))
+            for w in range(2):
+                a = PARTS[j][w]
+                nc.tensor.matmul_mx(
+                    out=acc[:],
+                    lhsT=qc[a, w][:, cols].bitcast(FP8X4),
+                    lhsT_scale=qs[a, w][:, cols],
+                    rhs=wdw[:, w, :].bitcast(FP4X4),
+                    rhs_scale=wds[:, w, :],
+                    start=(w == 0),
+                    stop=(w == 1),
+                )
+            nc.vector.tensor_tensor(out=zs[j][:, slot, :], in0=acc[:], in1=bdt[:], op=ADD)
+
+        bdc = kept([P, 4], F32, "bdc")
+
+        def bias_columns():
+            bank = ps2.tile([P, 4, P], BF16, name="bank2")
+            for c in range(4):
+                nc.tensor.transpose(bank[:, c, :], bdt[:, P * c : P * (c + 1)], identb[:])
+            turned["bd"] = bank
+
+        def bias_copy():
+            nc.vector.tensor_copy(out=bdc[:].unsqueeze(2), in_=turned["bd"][:, :, 0:1])
+
+        yt = {}
+
+        def decode_t(j):
+            made = outs.tile([P, 4, B], F32, name="yt", bufs=1)
+            yt[j] = made
+            for c in range(4):
+                acc = ps2.tile([P, B], F32, name="bank2")
+                for w in range(2):
+                    a = PARTS[j][w]
+                    nc.tensor.matmul_mx(
+                        out=acc[:],
+                        lhsT=wdw[:, w, 2 * P * c : 2 * P * (c + 1)].bitcast(FP4X4),
+                        lhsT_scale=wds[:, w, P * c : P * (c + 1)],
+                        rhs=qc[a, w][:].bitcast(FP8X4),
+                        rhs_scale=qs[a, w][:],
+                        start=(w == 0),
+                        stop=(w == 1),
+                    )
+                nc.scalar.activation(out=yt[j][:, c, :], in_=acc[:], func=ACT.Sigmoid, bias=bdc[:, c : c + 1])
+
+        ys = {}
+
+        def flip(j, i):
+            bank = ps2.tile([P, O], F32, name="bank2")
+            for c in range(4):
+                nc.tensor.transpose(bank[:, P * c : P * (c + 1)], yt[j][:, c, P * i : P * (i + 1)], ident[:])
+            if i % 2 == 0:
+                made = outs.tile([P, 2, O], F32, name="y")
+                ys[j] = made
+            nc.scalar.copy(out=ys[j][:, i % 2, :], in_=bank[:])
+            if i % 2 == 1:
+                store(ys[j], j, i - 1, 2)
+
+        def store(tile, j, i0, count):
+            nc.sync.dma_start(
+                out=out[j, P * i0 : P * (i0 + count), :].rearrange("(i q) o -> q i o", q=P), in_=tile[:, 0:count, :]
+            )
+
+        def finish(j, i0, count, slot):
+            y = outs.tile([P, 2, O], F32, name="y")
+            nc.scalar.activation(out=y[:, 0:count, :], in_=zs[j][:, slot : slot + count, :], func=ACT.Sigmoid)
+            store(y, j, i0, count)
+
+        widen(0, 0, 0, "v")
+        widen(0, 0, 1, "v")
+        turn(0, 0)
+        widen(0, 1, 0, "v")
+        widen(0, 1, 1, "v")
+        turn(0, 1)
+        empty(0, 0, "s")
+        empty(0, 1, "s")
+        interleave(0, 0, 2, "v")
+        interleave(0, 2, 4, "s")
+        quant_x(0, 0, 1)
+        quant_p(0, 0, 2)
+        quant_x(0, 1, 2)
+        quant_p(0, 2, 4)
+        for t in range(4):
+            project(0, 0, t, 0, 1)
+        interleave(1, 2, 4, "s")
+        for t in range(4):
+            project(0, 0, t, 1, 2)
+        interleave(1, 0, 2, "v")
+        widen(1, 0, 0, "v")
+        widen(1, 0, 1, "v")
+        gain(0, 0, 0)
+        quant_p(1, 0, 2)
+        quant_p(1, 2, 4)
+        for t in range(4):
+            project(0, 1, t, 0, 1)
+        turn(1, 0)
+        widen(1, 1, 0, "v")
+        widen(1, 1, 1, "v")
+        turn(1, 1)
+        gain(0, 0, 1)
+        empty(1, 0, "s")
+        empty(1, 1, "s")
+        for t in range(4):
+            project(0, 1, t, 1, 2)
+        gain(0, 1, 0)
+        quant_x(1, 0, 2)
+        quant_q(0, 0, 0, 2)
+        bias_columns()
+        for w in range(2):
+            for t in range(4):
+                project(1, w, t)
+        gain(0, 1, 1)
+        bias_copy()
+        quant_q(0, 1, 0, 1)
+        quant_q(0, 1, 1, 2)
+        gain(1, 0, 0)
+        gain(1, 0, 1)
+        decode_t(0)
+        quant_q(1, 0, 0, 1)
+        quant_q(1, 0, 1, 2)
+        gain(1, 1, 0)
+        decode(2, 0, 0)
+        decode(2, 1, 1)
+        flip(0, 0)
+        flip(0, 1)
+        finish(2, 0, 2, 0)
+        gain(1, 1, 1)
+        quant_q(1, 1, 0, 1)
+        decode(2, 2, 0)
+        quant_q(1, 1, 1, 2)
+        decode(2, 3, 1)
+        flip(0, 2)
+        flip(0, 3)
+        finish(2, 2, 2, 0)
+        for i in (0, 2):
+            for j in (1, 3):
+                decode(j, i, 0)
+                if (i, j) == (2, 3):
+                    finish(j, i, 1, 0)
+                decode(j, i + 1, 1)
+                if (i, j) == (2, 3):
+                    finish(j, i + 1, 1, 1)
+                else:
+                    finish(j, i, 2, 0)

@@ -42,23 +42,23 @@ def tile_switchtabmutualsalientswap_d2p_kernel(tc, x_bytes, x_scale, p, b, g, wd
             made = keep.tile(shape, dtype, name=label, align_bytes=64)
             return made
 
-        warm = kept([P, 1], F32, "warm")
-        nc.gpsimd.memset(warm[:], 0.0)
-        warmed = kept([P, 1], F32, "warmed")
-        nc.scalar.activation(out=warmed[:], in_=warm[:], func=ACT.Sigmoid)
-        ident = kept([P, P], F32, "ident")
-        make_identity(nc, ident[:])
-        identb = kept([P, P], BF16, "identb")
-        nc.gpsimd.tensor_copy(out=identb[:], in_=ident[:])
-        wds = kept([P, 2, O], U8, "wds")
-        nc.gpsimd.memset(wds[:].rearrange("q g n -> q (g n)").bitcast(I32), 0)
-
         xs = kept([P, V * 16], F32, "xs")
         nc.scalar.dma_start(out=xs[:], in_=x_scale.rearrange("a i j -> (a i j)").partition_broadcast(P))
         braw = kept([P, V, T4], BF16, "braw")
-        nc.gpsimd.dma_start(out=braw[:], in_=b.rearrange("a (q t) -> q a t", t=T4))
+        nc.scalar.dma_start(out=braw[:], in_=b.rearrange("a (q t) -> q a t", t=T4))
         graw = kept([P, 2, T4], BF16, "graw")
-        nc.gpsimd.dma_start(out=graw[:], in_=g.rearrange("(a q t) -> q a t", a=2, t=T4))
+        nc.scalar.dma_start(out=graw[:], in_=g.rearrange("(a q t) -> q a t", a=2, t=T4))
+
+        ident = kept([P, P], F32, "ident")
+        make_identity(nc, ident[:])
+        warm = kept([P, 1], F32, "warm")
+        nc.vector.memset(warm[:], 0.0)
+        warmed = kept([P, 1], F32, "warmed")
+        nc.scalar.activation(out=warmed[:], in_=warm[:], func=ACT.Sigmoid)
+        wds = kept([P, 2, O], U8, "wds")
+        nc.vector.memset(wds[:].rearrange("q g n -> q (g n)").bitcast(I32), 0)
+        identb = kept([P, P], BF16, "identb")
+        nc.vector.tensor_copy(out=identb[:], in_=ident[:])
 
         xb = {}
 
@@ -205,9 +205,9 @@ def tile_switchtabmutualsalientswap_d2p_kernel(tc, x_bytes, x_scale, p, b, g, wd
                 qg[a, w] = made
             rows = slice(256 * h, 256 * (h + 1))
             nc.vector.tensor_tensor(
-                out=qg[a, w][:, rows, :],
-                in0=th[a, w][:, :, rows].rearrange("q t n -> q n t"),
-                in1=gh[:, T4 * w : T4 * (w + 1)].unsqueeze(1).to_broadcast([P, 256, T4]),
+                out=qg[a, w][:, rows, :].rearrange("q (c i) t -> q c t i", i=4),
+                in0=th[a, w][:, :, rows].rearrange("q t (c i) -> q c t i", i=4),
+                in1=gh[:, T4 * w : T4 * (w + 1)].unsqueeze(1).unsqueeze(3).to_broadcast([P, 64, T4, 4]),
                 op=MULT,
             )
 

from contextlib import ExitStack

import concourse.mybir as mybir
from concourse.masks import make_identity

F32 = mybir.dt.float32
BF16 = mybir.dt.bfloat16
I32 = mybir.dt.int32
U32 = mybir.dt.uint32
U8 = mybir.dt.uint8
FP8 = mybir.dt.float8_e4m3fn
FP8X4 = mybir.dt.float8_e4m3fn_x4
FP4X4 = mybir.dt.float4_e2m1fn_x4
ACT = mybir.ActivationFunctionType
MULT = mybir.AluOpType.mult
ADD = mybir.AluOpType.add

P = 128
T4 = 4
V = 2
B = 512
D = 512
H = 512
O = 512
PARTS = ((0, 0), (1, 1), (1, 0), (0, 1))

FLOPS = 2 * (V * V * B * D * H + len(PARTS) * B * 2 * H * O)


def tile_switchtabmutualsalientswap_d2p_kernel(tc, x_bytes, x_scale, p, b, g, wd_words, wd_scales, bd, out):
    nc = tc.nc
    with ExitStack() as ctx:
        keep = ctx.enter_context(tc.tile_pool(name="keep", bufs=1))
        wide = ctx.enter_context(tc.tile_pool(name="wide", bufs=4))
        work = ctx.enter_context(tc.tile_pool(name="work", bufs=2))
        outs = ctx.enter_context(tc.tile_pool(name="outs", bufs=4))
        ps1 = ctx.enter_context(tc.psum_pool(name="ps1", bufs=4))
        ps2 = ctx.enter_context(tc.psum_pool(name="ps2", bufs=4))
        ctx.enter_context(tc.manual_schedule())

        def kept(shape, dtype, label):
            made = keep.tile(shape, dtype, name=label, align_bytes=64)
            return made

        xs = kept([P, V * 16], F32, "xs")
        nc.scalar.dma_start(out=xs[:], in_=x_scale.rearrange("a i j -> (a i j)").partition_broadcast(P))
        braw = kept([P, V, T4], BF16, "braw")
        nc.scalar.dma_start(out=braw[:], in_=b.rearrange("a (q t) -> q a t", t=T4))
        graw = kept([P, 2, T4], BF16, "graw")
        nc.scalar.dma_start(out=graw[:], in_=g.rearrange("(a q t) -> q a t", a=2, t=T4))

        ident = kept([P, P], F32, "ident")
        make_identity(nc, ident[:])
        warm = kept([P, 1], F32, "warm")
        nc.vector.memset(warm[:], 0.0)
        warmed = kept([P, 1], F32, "warmed")
        nc.scalar.activation(out=warmed[:], in_=warm[:], func=ACT.Sigmoid)
        wds = kept([P, 2, O], U8, "wds")
        nc.vector.memset(wds[:].rearrange("q g n -> q (g n)").bitcast(I32), 0)
        identb = kept([P, P], BF16, "identb")
        nc.vector.tensor_copy(out=identb[:], in_=ident[:])

        xb = {}

        def load_x(a, h):
            tile = kept([P, 2, D], U8, "xb%d%d" % (a, h))
            nc.sync.dma_start(out=tile[:], in_=x_bytes[a, 256 * h : 256 * (h + 1), :].rearrange("(i q) k -> q i k", q=P))
            xb[a, h] = tile

        praw = {}

        def load_p(w):
            tile = kept([P, T4, H], BF16, "praw%d" % w)
            nc.sync.dma_start(out=tile[:], in_=p[w].rearrange("(q j) c -> q j c", j=T4))
            praw[w] = tile

        load_x(0, 0)
        load_x(0, 1)
        load_p(0)
        load_p(1)
        load_x(1, 0)
        load_x(1, 1)
        wdw = kept([P, 2, 2 * O], U8, "wdw")
        nc.sync.dma_start(out=wdw[:].bitcast(I32), in_=wd_words.bitcast(I32).rearrange("g q n -> q g n"))
        for quad in range(4):
            nc.sync.dma_start(
                out=wds[32 * quad : 32 * quad + 4, :, :].bitcast(I32),
                in_=wd_scales[:, 4 * quad : 4 * quad + 4, :].bitcast(I32).rearrange("g q n -> q g n"),
            )
        bdt = kept([P, O], BF16, "bdt")
        nc.sync.dma_start(out=bdt[:], in_=bd.partition_broadcast(P))

        bh = kept([P, V * T4], F32, "bh")
        nc.gpsimd.tensor_scalar(out=bh[:], in0=braw[:].rearrange("q a t -> q (a t)"), scalar1=0.5, scalar2=0.0, op0=MULT, op1=ADD)
        gh = kept([P, 2 * T4], F32, "gh")
        nc.gpsimd.tensor_scalar(out=gh[:], in0=graw[:].rearrange("q a t -> q (a t)"), scalar1=0.5, scalar2=0.0, op0=MULT, op1=ADD)

        xw = {}
        xg = {}
        xc = {}
        xsc = {}
        pg = {}
        pc = {}
        psc = {}
        for a in range(V):
            xg[a] = kept([P, B, T4], BF16, "xg%d" % a)
            xc[a] = kept([P, B], U32, "xc%d" % a)
            xsc[a] = kept([P, B], U8, "xsc%d" % a)
            pg[a] = kept([P, T4 * P * T4], BF16, "pg%d" % a)
            pc[a] = kept([P, H], U32, "pc%d" % a)
            psc[a] = kept([P, H], U8, "psc%d" % a)
            for h in range(2):
                xw[a, h] = kept([P, 2, D], BF16, "xw%d%d" % (a, h))
        qc = {}
        qs = {}
        for a in range(V):
            for w in range(2):
                qc[a, w] = kept([P, B], U32, "qc%d%d" % (a, w))
                qs[a, w] = kept([P, B], U8, "qs%d%d" % (a, w))

        def widen(a, h, i, engine):
            for j in range(4):
                cols = slice(P * j, P * (j + 1))
                at = 16 * a + 4 * (2 * h + i) + j
                src = xb[a, h][:, i, cols].bitcast(FP8)
                dst = xw[a, h][:, i, cols]
                if engine == "v":
                    nc.vector.tensor_scalar(out=dst, in0=src, scalar1=xs[:, at : at + 1], scalar2=None, op0=MULT)
                else:
                    nc.scalar.activation(out=dst, in_=src, func=ACT.Copy, scale=xs[:, at : at + 1])

        turned = {}

        def turn(a, h):
            bank = ps2.tile([P, 2, 2, P], F32, name="bank2")
            for i in range(2):
                words = xw[a, h][:, i, :].bitcast(F32)
                for u in range(2):
                    nc.tensor.transpose(bank[:, i, u, :], words[:, u : D // 2 : 2], ident[:])
            turned[a, h] = bank

        def empty(a, h, engine):
            words = xg[a][:].rearrange("q n t -> q (n t)").bitcast(F32)
            dst = words[:, 512 * h : 512 * (h + 1)].rearrange("q (i r u) -> q i r u", i=2, u=2)
            src = turned[a, h][:].rearrange("q i u r -> q i r u")
            if engine == "v":
                nc.vector.tensor_copy(out=dst, in_=src)
            else:
                nc.scalar.copy(out=dst, in_=src)

        def quant_x(a, h0, h1):
            cols = slice(256 * h0, 256 * h1)
            nc.vector.quantize_mx(
                out=xc[a][:, cols].bitcast(FP8X4),
                scales=xsc[a][:, cols],
                in_=xg[a][:].rearrange("q n t -> q (n t)")[:, 1024 * h0 : 1024 * h1],
            )

        def interleave(w, t0, t1, engine):
            dst = pg[w][:].rearrange("q (t m j) -> q t m j", t=T4, j=T4)[:, t0:t1]
            src = praw[w][:].rearrange("q j (m t) -> q t m j", t=T4)[:, t0:t1]
            if engine == "v":
                nc.vector.tensor_copy(out=dst, in_=src)
            else:
                nc.scalar.copy(out=dst, in_=src)

        def quant_p(w, t0, t1):
            cols = slice(P * t0, P * t1)
            nc.vector.quantize_mx(
                out=pc[w][:, cols].bitcast(FP8X4), scales=psc[w][:, cols], in_=pg[w][:, T4 * P * t0 : T4 * P * t1]
            )

        th = {}

        def project(a, w, t, h0=0, h1=2):
            if t == 0 and h0 == 0:
                parts = wide.tile([P, T4, B], F32, name="th")
                th[a, w] = parts
            rows = slice(256 * h0, 256 * h1)
            acc = ps1.tile([P, B], F32, name="bank1")
            cols = slice(P * t, P * (t + 1))
            nc.tensor.matmul_mx(
                out=acc[:, 0 : 256 * (h1 - h0)],
                lhsT=pc[w][:, cols].bitcast(FP8X4),
                lhsT_scale=psc[w][:, cols],
                rhs=xc[a][:, rows].bitcast(FP8X4),
                rhs_scale=xsc[a][:, rows],
                start=True,
                stop=True,
            )
            at = T4 * w + t
            nc.scalar.activation(
                out=th[a, w][:, t, rows],
                in_=acc[:, 0 : 256 * (h1 - h0)],
                func=ACT.Tanh,
                bias=bh[:, at : at + 1],
                scale=0.5,
            )

        qg = {}

        def gain(a, w, h):
            if h == 0:
                made = work.tile([P, B, T4], BF16, name="qg", align_bytes=64)
                qg[a, w] = made
            rows = slice(256 * h, 256 * (h + 1))
            nc.vector.tensor_tensor(
                out=qg[a, w][:, rows, :].rearrange("q (c i) t -> q c t i", i=4),
                in0=th[a, w][:, :, rows].rearrange("q t (c i) -> q c t i", i=4),
                in1=gh[:, T4 * w : T4 * (w + 1)].unsqueeze(1).unsqueeze(3).to_broadcast([P, 64, T4, 4]),
                op=MULT,
            )

        def quant_q(a, w, h0, h1):
            cols = slice(256 * h0, 256 * h1)
            nc.vector.quantize_mx(
                out=qc[a, w][:, cols].bitcast(FP8X4),
                scales=qs[a, w][:, cols],
                in_=qg[a, w][:].rearrange("q n t -> q (n t)")[:, 1024 * h0 : 1024 * h1],
            )

        zs = {}

        def decode(j, i, slot):
            if slot == 0:
                made = outs.tile([P, 2, O], F32, name="z")
                zs[j] = made
            if j in (1, 3) and slot == 1:
                acc = ps1.tile([P, O], F32, name="bank1")
            else:
                acc = ps2.tile([P, O], F32, name="bank2")
            cols = slice(P * i, P * (i + 1))
            for w in range(2):
                a = PARTS[j][w]
                nc.tensor.matmul_mx(
                    out=acc[:],
                    lhsT=qc[a, w][:, cols].bitcast(FP8X4),
                    lhsT_scale=qs[a, w][:, cols],
                    rhs=wdw[:, w, :].bitcast(FP4X4),
                    rhs_scale=wds[:, w, :],
                    start=(w == 0),
                    stop=(w == 1),
                )
            nc.vector.tensor_tensor(out=zs[j][:, slot, :], in0=acc[:], in1=bdt[:], op=ADD)

        bdc = kept([P, 4], F32, "bdc")

        def bias_columns():
            bank = ps2.tile([P, 4, P], BF16, name="bank2")
            for c in range(4):
                nc.tensor.transpose(bank[:, c, :], bdt[:, P * c : P * (c + 1)], identb[:])
            turned["bd"] = bank

        def bias_copy():
            nc.vector.tensor_copy(out=bdc[:].unsqueeze(2), in_=turned["bd"][:, :, 0:1])

        yt = {}

        def decode_t(j):
            made = outs.tile([P, 4, B], F32, name="yt", bufs=1)
            yt[j] = made
            for c in range(4):
                acc = ps2.tile([P, B], F32, name="bank2")
                for w in range(2):
                    a = PARTS[j][w]
                    nc.tensor.matmul_mx(
                        out=acc[:],
                        lhsT=wdw[:, w, 2 * P * c : 2 * P * (c + 1)].bitcast(FP4X4),
                        lhsT_scale=wds[:, w, P * c : P * (c + 1)],
                        rhs=qc[a, w][:].bitcast(FP8X4),
                        rhs_scale=qs[a, w][:],
                        start=(w == 0),
                        stop=(w == 1),
                    )
                nc.scalar.activation(out=yt[j][:, c, :], in_=acc[:], func=ACT.Sigmoid, bias=bdc[:, c : c + 1])

        ys = {}

        def flip(j, i):
            bank = ps2.tile([P, O], F32, name="bank2")
            for c in range(4):
                nc.tensor.transpose(bank[:, P * c : P * (c + 1)], yt[j][:, c, P * i : P * (i + 1)], ident[:])
            if i % 2 == 0:
                made = outs.tile([P, 2, O], F32, name="y")
                ys[j] = made
            nc.scalar.copy(out=ys[j][:, i % 2, :], in_=bank[:])
            if i % 2 == 1:
                store(ys[j], j, i - 1, 2)

        def store(tile, j, i0, count):
            nc.sync.dma_start(
                out=out[j, P * i0 : P * (i0 + count), :].rearrange("(i q) o -> q i o", q=P), in_=tile[:, 0:count, :]
            )

        def finish(j, i0, count, slot):
            y = outs.tile([P, 2, O], F32, name="y")
            nc.scalar.activation(out=y[:, 0:count, :], in_=zs[j][:, slot : slot + count, :], func=ACT.Sigmoid)
            store(y, j, i0, count)

        widen(0, 0, 0, "v")
        widen(0, 0, 1, "v")
        turn(0, 0)
        widen(0, 1, 0, "v")
        widen(0, 1, 1, "v")
        turn(0, 1)
        empty(0, 0, "s")
        empty(0, 1, "s")
        interleave(0, 0, 2, "v")
        interleave(0, 2, 4, "s")
        quant_x(0, 0, 1)
        quant_p(0, 0, 2)
        quant_x(0, 1, 2)
        quant_p(0, 2, 4)
        for t in range(4):
            project(0, 0, t, 0, 1)
        interleave(1, 2, 4, "s")
        for t in range(4):
            project(0, 0, t, 1, 2)
        interleave(1, 0, 2, "v")
        widen(1, 0, 0, "v")
        widen(1, 0, 1, "v")
        gain(0, 0, 0)
        quant_p(1, 0, 2)
        quant_p(1, 2, 4)
        for t in range(4):
            project(0, 1, t, 0, 1)
        turn(1, 0)
        widen(1, 1, 0, "v")
        widen(1, 1, 1, "v")
        turn(1, 1)
        gain(0, 0, 1)
        empty(1, 0, "s")
        empty(1, 1, "s")
        for t in range(4):
            project(0, 1, t, 1, 2)
        gain(0, 1, 0)
        quant_x(1, 0, 2)
        quant_q(0, 0, 0, 2)
        bias_columns()
        for w in range(2):
            for t in range(4):
                project(1, w, t)
        gain(0, 1, 1)
        bias_copy()
        quant_q(0, 1, 0, 1)
        quant_q(0, 1, 1, 2)
        gain(1, 0, 0)
        gain(1, 0, 1)
        decode_t(0)
        quant_q(1, 0, 0, 1)
        quant_q(1, 0, 1, 2)
        gain(1, 1, 0)
        decode(2, 0, 0)
        decode(2, 1, 1)
        flip(0, 0)
        flip(0, 1)
        finish(2, 0, 2, 0)
        gain(1, 1, 1)
        quant_q(1, 1, 0, 1)
        decode(2, 2, 0)
        quant_q(1, 1, 1, 2)
        decode(2, 3, 1)
        flip(0, 2)
        flip(0, 3)
        finish(2, 2, 2, 0)
        for i in (0, 2):
            for j in (1, 3):
                decode(j, i, 0)
                if (i, j) == (2, 3):
                    finish(j, i, 1, 0)
                decode(j, i + 1, 1)
                if (i, j) == (2, 3):
                    finish(j, i + 1, 1, 1)
                else:
                    finish(j, i, 2, 0)
